import numpy as np
import ml_dtypes


def mxq(x, axis, fmt="e4m3"):
    dtype, down = {"e4m3": (ml_dtypes.float8_e4m3fn, 7), "e5m2": (ml_dtypes.float8_e5m2, 14)}[fmt]
    v = np.moveaxis(np.asarray(x, np.float32).astype(ml_dtypes.bfloat16).astype(np.float64), axis, -1)
    blocks = v.reshape(v.shape[:-1] + (-1, 32))
    amax = np.abs(blocks).max(-1, keepdims=True)
    byte = np.maximum(np.where(amax > 0, np.frexp(amax)[1] - 1 + 127, 0) - down, 1)
    scale = np.exp2(byte - 127.0)
    codes = (blocks / scale).astype(np.float32).astype(dtype).astype(np.float64)
    return np.moveaxis((codes * scale).reshape(v.shape), -1, axis)


WIDE = False


def mx_kscale(k):
    if not WIDE:
        return np.ones(k)
    levels = np.array([10, -10, 5, -5, 0])
    if k % 512:
        return np.exp2(np.random.permutation(np.resize(levels, k // 32))).repeat(32)
    a = np.empty((k // 512, 16))
    for p in range(k // 512):
        a[p, :8] = np.random.permutation(np.resize(levels, 8))
        for g in range(8):
            far = levels[np.abs(levels - a[p, g]) >= 10]
            a[p, g + 8] = far[np.random.randint(len(far))]
    return np.exp2(a.ravel()).repeat(32)


def f64(x):
    return np.asarray(x).astype(np.float64)


def striped(idx):
    return np.tile(idx.reshape(-1, 16).T, (8, 1)).astype(np.uint16)


def unstriped(offs):
    return offs[:16].T.reshape(-1).astype(np.int64)


E2M1 = np.array([0.0, 0.5, 1.0, 1.5, 2.0, 3.0, 4.0, 6.0, -0.0, -0.5, -1.0, -1.5, -2.0, -3.0, -4.0, -6.0])


def pack_weight(w, fmt):
    k, n = w.shape
    w = f64(np.asarray(w, np.float32).astype(ml_dtypes.bfloat16)).reshape(k // 32, 32, n)
    amax = np.abs(w).max(1)
    if fmt == "e4m3":
        byte = np.frexp(amax)[1] - 1 + 127 - 7
    else:
        mant, ex = np.frexp(amax / 6.0)
        byte = np.where(mant > 0.5, ex, ex - 1) + 127
    byte = np.clip(np.where(amax > 0, byte, 1), 1, 254)
    scaled = (w * np.exp2(127.0 - byte)[:, None, :]).reshape(k, n).astype(np.float32)
    by_word = np.ascontiguousarray(scaled.reshape(k // 512, 128, 4, n).transpose(0, 1, 3, 2))
    if fmt == "e4m3":
        words = by_word.astype(ml_dtypes.float8_e4m3fn).view(np.uint8)
    else:
        c = by_word.astype(ml_dtypes.float4_e2m1fn).view(np.uint8) & 0xF
        words = (c[..., 0::2] | (c[..., 1::2] << 4)).reshape(k // 512, 128, 2 * n)
    return np.ascontiguousarray(words), np.ascontiguousarray(byte.astype(np.uint8).reshape(k // 512, 16, n))


def unpack_weight(words, scales, fmt):
    g, _, n = scales.shape
    words = np.ascontiguousarray(words).reshape(g, 128, n, -1)
    if fmt == "e4m3":
        vals = words.view(ml_dtypes.float8_e4m3fn).astype(np.float64)
    else:
        nib = np.empty((g, 128, n, 4), np.uint8)
        nib[..., 0::2] = words & 0xF
        nib[..., 1::2] = words >> 4
        vals = E2M1[nib]
    vals = vals * np.repeat(np.exp2(scales.astype(np.float64) - 127.0), 8, axis=1)[..., None]
    return vals.transpose(0, 1, 3, 2).reshape(g * 512, n)


def gelu(v):
    return 0.5 * v * (1.0 + np.tanh(np.sqrt(2.0 / np.pi) * (v + 0.044715 * v**3)))


def often(T, S):
    return np.random.permutation(T)[(T * np.random.uniform(0, 1, S) ** 4).astype(np.int64)]


K, K2, H, N, T, S, P = 1024, 512, 1024, 512, 2048, 1024, 512

def setup_inputs():
    n = np.random.standard_normal
    s = mx_kscale(K)[:, None]
    s2 = mx_kscale(K2)[:, None]
    u = mx_kscale(H)[:, None]
    d = {}
    d["tab_words"], d["tab_scales"] = pack_weight(n((K, T)) * s, "e4m3")
    d["tab2_words"], d["tab2_scales"] = pack_weight(n((K2, T)) * s2, "e4m3")
    d["tab3_words"], d["tab3_scales"] = pack_weight(n((K2, T)) * s2, "e4m3")
    d["offs"] = striped(np.random.permutation(T)[:S])
    d["offs2"] = striped(np.random.permutation(T)[:S])
    d["offs3"] = striped(np.random.permutation(T)[:S])
    d["pos1"] = striped(np.random.permutation(S)[:P])
    d["pos2"] = striped(often(S, P))
    d["pos3"] = striped(often(S, P))
    d["w1"] = (n((K, H)) / K ** 0.5 / s * u.T).astype(np.float32)
    d["w2_words"], d["w2_scales"] = pack_weight(n((K2, H)) / K2 ** 0.5 / s2 * u.T, "e2m1")
    d["w3"] = (n((K2, H)) / K2 ** 0.5 / s2).astype(np.float32)
    d["bd"] = (0.5 * n(H)).astype(np.float32)
    d["w4"] = (n((H, N)) / H ** 0.5 / u).astype(np.float32)
    d["w5_words"], d["w5_scales"] = pack_weight(n((H, N)) / H ** 0.5 / u, "e2m1")
    d["ge"] = np.exp(0.3 * n(N)).astype(np.float32)
    return d

def reference(tab_words, tab_scales, tab2_words, tab2_scales, tab3_words, tab3_scales, offs, offs2, offs3,
              pos1, pos2, pos3, w1, w2_words, w2_scales, w3, bd, w4, w5_words, w5_scales, ge):
    v = unpack_weight(tab_words, tab_scales, "e4m3")[:, unstriped(offs)]
    v2 = unpack_weight(tab2_words, tab2_scales, "e4m3")[:, unstriped(offs2)]
    v3 = unpack_weight(tab3_words, tab3_scales, "e4m3")[:, unstriped(offs3)]
    a = mxq(f64(w1), 0, "e4m3").T @ v
    b = unpack_weight(w2_words, w2_scales, "e2m1").T @ v2
    d = (mxq(f64(w3), 0, "e4m3").T @ v3) + f64(bd)[:, None]
    xb = b[:, unstriped(pos2)]
    z = np.maximum(a[:, unstriped(pos1)], xb) * d[:, unstriped(pos3)]
    y1 = mxq(f64(w4), 0, "e4m3").T @ mxq(z, 0, "e4m3")
    y2 = unpack_weight(w5_words, w5_scales, "e2m1").T @ mxq(xb, 0, "e4m3")
    return np.square(y1 - f64(ge)[:, None] * y2)

@@ -1,0 +1,302 @@
+from contextlib import ExitStack
+
+import concourse.mybir as mybir
+
+K, K2, H, N, T, S, J = 1024, 512, 1024, 512, 2048, 1024, 512
+FLOPS = 2 * (K * H * S + 2 * K2 * H * S + 2 * H * N * J)
+
+F32 = mybir.dt.float32
+BF16 = mybir.dt.bfloat16
+I32 = mybir.dt.int32
+U32 = mybir.dt.uint32
+U16 = mybir.dt.uint16
+U8 = mybir.dt.uint8
+FP8X4 = mybir.dt.float8_e4m3fn_x4
+FP4X4 = mybir.dt.float4_e2m1fn_x4
+ACT = mybir.ActivationFunctionType
+ALU = mybir.AluOpType
+
+P = 128
+PACK = 4
+PASS = P * PACK
+BANK = 512
+HALF = J // 2
+
+
+def tile_list_emergency_call_desk_kernel(
+    tc, tab_words, tab_scales, tab2_words, tab2_scales, tab3_words, tab3_scales,
+    offs, offs2, offs3, pos1, pos2, pos3, w1, w2_words, w2_scales, w3, bd, w4,
+    w5_words, w5_scales, ge, out,
+):
+    nc = tc.nc
+    with ExitStack() as ctx:
+        keep = ctx.enter_context(tc.tile_pool(name="keep", bufs=1))
+        raws = ctx.enter_context(tc.tile_pool(name="raws", bufs=1))
+        woven = ctx.enter_context(tc.tile_pool(name="woven", bufs=1))
+        rows = ctx.enter_context(tc.tile_pool(name="rows", bufs=1))
+        results = ctx.enter_context(tc.tile_pool(name="results", bufs=3))
+        acc_pool = ctx.enter_context(tc.psum_pool(name="acc", bufs=1))
+        y_pool = ctx.enter_context(tc.psum_pool(name="y", bufs=2))
+
+        made = {"row": 0, "acc": 0}
+
+        def in_turn(pool, kind, slots, shape):
+            n = made[kind]
+            made[kind] = n + 1
+            return pool.tile(shape, F32, name="%s%d" % (kind, n % slots))
+
+        def load_list(name, src):
+            tile = keep.tile(list(src.shape), U16, name=name)
+            nc.sync.dma_start(tile[:], src)
+            return tile
+
+        def zeroed_plane(name, width):
+            plane = keep.tile([P, width], U8, name=name, align_bytes=64)
+            nc.vector.memset(plane[:].bitcast(I32), 0)
+            return plane
+
+        def load_table_scales(plane, scales):
+            passes = scales.shape[0]
+            for q in range(4):
+                nc.sync.dma_start(
+                    out=plane[32 * q : 32 * q + 4 * passes, :].bitcast(I32),
+                    in_=scales[:, 4 * q : 4 * q + 4, :].bitcast(I32),
+                )
+
+        def load_table_words(name, words):
+            tile = keep.tile([P, T], I32, name=name)
+            nc.sync.dma_start(out=tile[:], in_=words.rearrange("p t i -> p (t i)").bitcast(I32))
+            return tile
+
+        def gather_words(name, words, idx):
+            picked = keep.tile([P, S], U32, name=name, align_bytes=64)
+            nc.vector.tensor_copy(picked[:], words[:].bitcast(U32).indirect(idx[:]))
+            return picked
+
+        def gather_scales(name, plane, idx):
+            picked = keep.tile([P, S], U8, name=name, align_bytes=64)
+            nc.vector.tensor_copy(picked[:], plane[:].indirect(idx[:]))
+            return picked
+
+        def load_weight_block(w, a, b, slot):
+            raw = raws.tile([P, PACK, PASS], F32, name="raw%d" % slot)
+            nc.sync.dma_start(
+                out=raw[:],
+                in_=w[PASS * a : PASS * (a + 1), PASS * b : PASS * (b + 1)].rearrange("(p j) c -> p j c", j=PACK),
+            )
+            return raw
+
+        def quantize(name, bf, width):
+            codes = keep.tile([P, width], U32, name=name + "_codes", align_bytes=64)
+            scales = keep.tile([P, width], U8, name=name + "_scales", align_bytes=64)
+            nc.vector.quantize_mx(out=codes[:].bitcast(FP8X4), scales=scales[:], in_=bf)
+            return codes, scales
+
+        def weave_dealt(raw, slot):
+            bf = woven.tile([P, PACK * PASS], BF16, name="bf%d" % slot, align_bytes=64)
+            nc.scalar.copy(
+                out=bf[:].rearrange("p (t m j) -> p m j t", t=PACK, j=PACK),
+                in_=raw[:].rearrange("p j (m t) -> p m j t", t=PACK),
+            )
+            return bf[:]
+
+        def weave(copy, planes, width, slot):
+            bf = woven.tile([P, PACK * width], BF16, name="bf%d" % slot, align_bytes=64)
+            copy(
+                out=bf[:].rearrange("p (c i j) -> p c j i", i=4, j=PACK),
+                in_=planes.rearrange("p j (c i) -> p c j i", i=4),
+            )
+            return bf[:]
+
+        def first_stage(passes, bias, slot):
+            row = rows.tile([P, S], F32, name="row%d" % slot)
+            for c in range(S // BANK):
+                cols = slice(BANK * c, BANK * (c + 1))
+                acc = in_turn(acc_pool, "acc", 6, [P, BANK])
+                for n, (w_codes, w_scales, v_codes, v_scales, k) in enumerate(passes):
+                    nc.tensor.matmul_mx(
+                        out=acc[:], lhsT=w_codes, lhsT_scale=w_scales,
+                        rhs=v_codes[:, cols].bitcast(FP8X4), rhs_scale=v_scales[k:P, cols],
+                        start=(n == 0), stop=(n == len(passes) - 1),
+                    )
+                if bias is None:
+                    nc.scalar.copy(out=row[:, cols], in_=acc[:])
+                else:
+                    nc.scalar.activation(out=row[:, cols], in_=acc[:], func=ACT.Identity, bias=bias)
+            return row
+
+        def fp8_cols(q, u):
+            cols = slice(P * u, P * (u + 1))
+            return q[0][:, cols].bitcast(FP8X4), q[1][:, cols]
+
+        v2_plane = zeroed_plane("v2_plane", T)
+        w2_plane = zeroed_plane("w2_plane", H)
+        v3_plane = zeroed_plane("v3_plane", T)
+        v1_plane = zeroed_plane("v1_plane", T)
+        w5_plane = zeroed_plane("w5_plane", 2 * N)
+
+        idx2 = load_list("idx2", offs2)
+        idx3 = load_list("idx3", offs3)
+        w2_raw = keep.tile([P, 2 * H], U8, name="w2_raw")
+        nc.sync.dma_start(out=w2_raw[:].bitcast(I32), in_=w2_words[0].bitcast(I32))
+        load_table_scales(v2_plane, tab2_scales)
+        v2_words = load_table_words("v2_words", tab2_words[0])
+        w3_raw0 = load_weight_block(w3, 0, 0, 0)
+        load_table_scales(w2_plane, w2_scales)
+        v3_words = load_table_words("v3_words", tab3_words[0])
+        load_table_scales(v3_plane, tab3_scales)
+        w3_raw1 = load_weight_block(w3, 0, 1, 1)
+        p2 = load_list("p2", pos2)
+        v1_words = [load_table_words("v1_words0", tab_words[0])]
+        idx1 = load_list("idx1", offs)
+        load_table_scales(v1_plane, tab_scales)
+        v1_words.append(load_table_words("v1_words1", tab_words[1]))
+        bd_t = keep.tile([P, 2, PACK], F32, name="bd_t")
+        nc.sync.dma_start(out=bd_t[:], in_=bd.rearrange("(a p t) -> p a t", a=2, t=PACK))
+        w1_raw = {(a, 0): load_weight_block(w1, a, 0, 2 + a) for a in range(2)}
+        p1 = load_list("p1", pos1)
+        p3 = load_list("p3", pos3)
+
+        v2_scales = gather_scales("v2_scales", v2_plane, idx2)
+        w2_dealt = keep.tile([P, 2 * H], U8, name="w2_dealt", align_bytes=64)
+        nc.vector.tensor_copy(
+            out=w2_dealt[:].rearrange("p (b t m e) -> p b t m e", b=2, t=PACK, e=2),
+            in_=w2_raw[:].rearrange("p (b m t e) -> p b t m e", b=2, t=PACK, e=2),
+        )
+        v2_codes = gather_words("v2_codes", v2_words, idx2)
+        w2_dealt_scales = keep.tile([P, H], U8, name="w2_dealt_scales", align_bytes=64)
+        nc.vector.tensor_copy(
+            out=w2_dealt_scales[:].rearrange("p (b t m) -> p b t m", b=2, t=PACK),
+            in_=w2_plane[:].rearrange("p (b m t) -> p b t m", b=2, t=PACK),
+        )
+        w3_bf = [weave_dealt(w3_raw0, 0), weave_dealt(w3_raw1, 1)]
+        for a in range(2):
+            w1_raw[(a, 1)] = load_weight_block(w1, a, 1, a)
+        w5_codes = keep.tile([P, 2, 2 * N], U8, name="w5_codes", align_bytes=64)
+        nc.sync.dma_start(out=w5_codes[:].bitcast(I32), in_=w5_words.rearrange("a p c -> p a c").bitcast(I32))
+        for q in range(4):
+            nc.sync.dma_start(
+                out=w5_plane[32 * q : 32 * q + 4, :].rearrange("r (a n) -> r a n", a=2).bitcast(I32),
+                in_=w5_scales[:, 4 * q : 4 * q + 4, :].rearrange("a r n -> r a n").bitcast(I32),
+            )
+        ge_t = keep.tile([P, N // P], F32, name="ge_t")
+        with nc.allow_non_contiguous_dma(reason="one gain a partition"):
+            nc.sync.dma_start(out=ge_t[:], in_=ge.rearrange("(i p) -> p i", p=P))
+
+        b_rows = [
+            first_stage(
+                [(w2_dealt[:, 2 * P * u : 2 * P * (u + 1)].bitcast(FP4X4), w2_dealt_scales[:, P * u : P * (u + 1)],
+                  v2_codes, v2_scales, 0)],
+                None, u,
+            )
+            for u in range(8)
+        ]
+
+        v3_scales = gather_scales("v3_scales", v3_plane, idx3)
+        v3_codes = gather_words("v3_codes", v3_words, idx3)
+        w3_q = [quantize("w3_%d" % b, w3_bf[b], PASS) for b in range(2)]
+        v1_scales = gather_scales("v1_scales", v1_plane, idx1)
+        v1_codes = [gather_words("v1_codes%d" % a, v1_words[a], idx1) for a in range(2)]
+
+        w1_q = {}
+        for a in range(2):
+            w1_q[(a, 0)] = quantize("w1_%d0" % a, weave_dealt(w1_raw[(a, 0)], 2 + a), PASS)
+        w4_raw = [load_weight_block(w4, 0, 0, 2)]
+
+        xb = [keep.tile([P, PACK, J], F32, name="xb0"), raws.tile([P, PACK, J], F32, name="raw3")]
+        for u in range(8):
+            nc.vector.tensor_copy(xb[u // PACK][:, u % PACK, :], b_rows[u][:].indirect(p2[:]))
+
+        def d_stage(u, slot):
+            b, t = divmod(u, PACK)
+            return first_stage([fp8_cols(w3_q[b], t) + (v3_codes, v3_scales, 0)], bd_t[:, b, t : t + 1], slot)
+
+        def a_stage(u, slot):
+            b, t = divmod(u, PACK)
+            return first_stage(
+                [fp8_cols(w1_q[(a, b)], t) + (v1_codes[a], v1_scales, 4 * a) for a in range(2)], None, slot
+            )
+
+        def pick_max(xa, b, j0, width):
+            for t in range(PACK):
+                nc.vector.tensor_copy(xa[:, t, :], a_rows[PACK * b + t][:].indirect(p1[:, j0 // 16 : (j0 + width) // 16]))
+            nc.vector.tensor_tensor(xa[:], xa[:], xb[b][:, :, j0 : j0 + width], ALU.max)
+
+        def pick_mult(z, xa, u, j0, width):
+            t = u % PACK
+            nc.vector.tensor_tensor(
+                z[:, t, :], d_rows[u][:].indirect(p3[:, j0 // 16 : (j0 + width) // 16]), xa[:, t, j0 : j0 + width], ALU.mult
+            )
+
+        z0 = keep.tile([P, PACK, J], F32, name="z0")
+        xa0 = keep.tile([P, PACK, J], F32, name="xa")
+        a_rows, d_rows = {}, {}
+        for u in range(2):
+            d_rows[u] = d_stage(u, 8 + u)
+        for u in range(4):
+            a_rows[u] = a_stage(u, u)
+        pick_max(xa0, 0, 0, J)
+        for u in range(2):
+            pick_mult(z0, xa0, u, 0, J)
+        for a in range(2):
+            w1_q[(a, 1)] = quantize("w1_%d1" % a, weave_dealt(w1_raw[(a, 1)], a), PASS)
+        w4_raw.append(load_weight_block(w4, 1, 0, 0))
+        for u in range(2, 4):
+            d_rows[u] = d_stage(u, 2 + u)
+            pick_mult(z0, xa0, u, 0, J)
+        w4_q = [quantize("w4_0", weave(nc.vector.tensor_copy, w4_raw[0][:], N, 3), N)]
+        for u in range(4, 8):
+            d_rows[u] = d_stage(u, (u + 2) % 8)
+        for u, slot in zip(range(4, 8), (2, 3, 8, 9)):
+            a_rows[u] = a_stage(u, slot)
+        xa1 = keep.tile([P, PACK, J], F32, name="xa")
+        pick_max(xa1, 1, 0, J)
+        xb_q = [quantize("xb_%d" % a, weave(nc.scalar.copy, xb[a][:], J, a), J) for a in range(2)]
+        z1 = [keep.tile([P, PACK, HALF], F32, name="z1_%d" % h) for h in range(2)]
+        for h in range(2):
+            for u in range(4, 8):
+                pick_mult(z1[h], xa1, u, HALF * h, HALF)
+        w4_q.append(quantize("w4_1", weave(nc.scalar.copy, w4_raw[1][:], N, 2), N))
+        z0_q = quantize("z0", weave(nc.scalar.copy, z0[:], J, 3), J)
+        z1_q = [quantize("z1_0", weave(nc.scalar.copy, z1[0][:], HALF, 0), HALF)]
+        y2 = keep.tile([P, N // P, J], F32, name="y2")
+        for i in range(N // P):
+            acc = in_turn(acc_pool, "acc", 6, [P, BANK])
+            for a in range(2):
+                nc.tensor.matmul_mx(
+                    out=acc[:],
+                    lhsT=w5_codes[:, a, 2 * P * i : 2 * P * (i + 1)].bitcast(FP4X4),
+                    lhsT_scale=w5_plane[:, N * a + P * i : N * a + P * (i + 1)],
+                    rhs=xb_q[a][0][:].bitcast(FP8X4), rhs_scale=xb_q[a][1][:],
+                    start=(a == 0), stop=(a == 1),
+                )
+            nc.scalar.activation(out=y2[:, i, :], in_=acc[:], func=ACT.Copy, scale=ge_t[:, i : i + 1])
+
+        z1_q.append(quantize("z1_1", weave(nc.scalar.copy, z1[1][:], HALF, 1), HALF))
+        out_v = out.rearrange("(i p) j -> p i j", p=P)
+
+        def finish(h):
+            cols = slice(HALF * h, HALF * (h + 1))
+            for pair in range(2):
+                y1 = y_pool.tile([P, 2, HALF], F32, name="y1")
+                for e in range(2):
+                    i = 2 * pair + e
+                    w_codes, w_scales = fp8_cols(w4_q[0], i)
+                    nc.tensor.matmul_mx(
+                        out=y1[:, e, :], lhsT=w_codes, lhsT_scale=w_scales,
+                        rhs=z0_q[0][:, cols].bitcast(FP8X4), rhs_scale=z0_q[1][:, cols],
+                        start=True, stop=False,
+                    )
+                    w_codes, w_scales = fp8_cols(w4_q[1], i)
+                    nc.tensor.matmul_mx(
+                        out=y1[:, e, :], lhsT=w_codes, lhsT_scale=w_scales,
+                        rhs=z1_q[h][0][:].bitcast(FP8X4), rhs_scale=z1_q[h][1][:],
+                        start=False, stop=True,
+                    )
+                diff = results.tile([P, 2, HALF], F32, name="diff")
+                nc.vector.tensor_tensor(diff[:], y1[:], y2[:, 2 * pair : 2 * pair + 2, cols], ALU.subtract)
+                nc.scalar.activation(out=diff[:], in_=diff[:], func=ACT.Square)
+                nc.sync.dma_start(out=out_v[:, 2 * pair : 2 * pair + 2, cols], in_=diff[:])
+
+        for h in range(2):
+            finish(h)

@@ -160,8 +160,8 @@ def tile_list_emergency_call_desk_kernel(
         v2_scales = gather_scales("v2_scales", v2_plane, idx2)
         w2_dealt = keep.tile([P, 2 * H], U8, name="w2_dealt", align_bytes=64)
         nc.vector.tensor_copy(
-            out=w2_dealt[:].rearrange("p (b t m e) -> p b t m e", b=2, t=PACK, e=2),
-            in_=w2_raw[:].rearrange("p (b m t e) -> p b t m e", b=2, t=PACK, e=2),
+            out=w2_dealt[:].bitcast(U16).rearrange("p (b t m) -> p b t m", b=2, t=PACK),
+            in_=w2_raw[:].bitcast(U16).rearrange("p (b m t) -> p b t m", b=2, t=PACK),
         )
         v2_codes = gather_words("v2_codes", v2_words, idx2)
         w2_dealt_scales = keep.tile([P, H], U8, name="w2_dealt_scales", align_bytes=64)
@@ -231,34 +231,24 @@ def tile_list_emergency_call_desk_kernel(
         z0 = keep.tile([P, PACK, J], F32, name="z0")
         xa0 = keep.tile([P, PACK, J], F32, name="xa")
         a_rows, d_rows = {}, {}
-        for u in range(2):
-            d_rows[u] = d_stage(u, 8 + u)
-        for u in range(4):
-            a_rows[u] = a_stage(u, u)
-        pick_max(xa0, 0, 0, J)
-        for u in range(2):
-            pick_mult(z0, xa0, u, 0, J)
+        for u, slot in zip(range(4), (8, 9, 0, 1)):
+            d_rows[u] = d_stage(u, slot)
         for a in range(2):
             w1_q[(a, 1)] = quantize("w1_%d1" % a, weave_dealt(w1_raw[(a, 1)], a), PASS)
         w4_raw.append(load_weight_block(w4, 1, 0, 0))
-        for u in range(2, 4):
-            d_rows[u] = d_stage(u, 2 + u)
+        for u in range(4):
+            a_rows[u] = a_stage(u, 2 + u)
+        w4_q = [quantize("w4_%d" % a, weave(nc.vector.tensor_copy, w4_raw[a][:], N, 3 - a), N) for a in range(2)]
+        pick_max(xa0, 0, 0, J)
+        xb_q = [quantize("xb_%d" % a, weave(nc.scalar.copy, xb[a][:], J, a), J) for a in range(2)]
+        for u in range(4):
             pick_mult(z0, xa0, u, 0, J)
-        w4_q = [quantize("w4_0", weave(nc.vector.tensor_copy, w4_raw[0][:], N, 3), N)]
-        for u in range(4, 8):
-            d_rows[u] = d_stage(u, (u + 2) % 8)
-        for u, slot in zip(range(4, 8), (2, 3, 8, 9)):
+        for u, slot in zip(range(4, 8), (6, 7, 2, 3)):
             a_rows[u] = a_stage(u, slot)
         xa1 = keep.tile([P, PACK, J], F32, name="xa")
         pick_max(xa1, 1, 0, J)
-        xb_q = [quantize("xb_%d" % a, weave(nc.scalar.copy, xb[a][:], J, a), J) for a in range(2)]
-        z1 = [keep.tile([P, PACK, HALF], F32, name="z1_%d" % h) for h in range(2)]
-        for h in range(2):
-            for u in range(4, 8):
-                pick_mult(z1[h], xa1, u, HALF * h, HALF)
-        w4_q.append(quantize("w4_1", weave(nc.scalar.copy, w4_raw[1][:], N, 2), N))
-        z0_q = quantize("z0", weave(nc.scalar.copy, z0[:], J, 3), J)
-        z1_q = [quantize("z1_0", weave(nc.scalar.copy, z1[0][:], HALF, 0), HALF)]
+        for u, slot in zip(range(4, 8), (4, 5, 8, 9)):
+            d_rows[u] = d_stage(u, slot)
         y2 = keep.tile([P, N // P, J], F32, name="y2")
         for i in range(N // P):
             acc = in_turn(acc_pool, "acc", 6, [P, BANK])
@@ -272,12 +262,19 @@ def tile_list_emergency_call_desk_kernel(
                 )
             nc.scalar.activation(out=y2[:, i, :], in_=acc[:], func=ACT.Copy, scale=ge_t[:, i : i + 1])
 
-        z1_q.append(quantize("z1_1", weave(nc.scalar.copy, z1[1][:], HALF, 1), HALF))
+        z0_q = quantize("z0", weave(nc.scalar.copy, z0[:], J, 3), J)
+        z1 = [keep.tile([P, PACK, HALF], F32, name="z1"), keep.tile([P, PACK, HALF], F32, name="z0")]
+        for u in range(4, 8):
+            pick_mult(z1[0], xa1, u, 0, HALF)
+        z1_q = [quantize("z1_0", weave(nc.scalar.copy, z1[0][:], HALF, 0), HALF)]
+        for u in range(4, 8):
+            pick_mult(z1[1], xa1, u, HALF, HALF)
+        last_bf = weave(nc.vector.tensor_copy, z1[1][:], HALF, 1)
         out_v = out.rearrange("(i p) j -> p i j", p=P)
 
-        def finish(h):
+        def finish(h, pair):
             cols = slice(HALF * h, HALF * (h + 1))
-            for pair in range(2):
+            if True:
                 y1 = y_pool.tile([P, 2, HALF], F32, name="y1")
                 for e in range(2):
                     i = 2 * pair + e
@@ -298,5 +295,8 @@ def tile_list_emergency_call_desk_kernel(
                 nc.scalar.activation(out=diff[:], in_=diff[:], func=ACT.Square)
                 nc.sync.dma_start(out=out_v[:, 2 * pair : 2 * pair + 2, cols], in_=diff[:])
 
-        for h in range(2):
-            finish(h)
+        finish(0, 0)
+        z1_q.append(quantize("z1_1", last_bf, HALF))
+        finish(0, 1)
+        for pair in range(2):
+            finish(1, pair)

@@ -108,6 +108,14 @@ def tile_list_emergency_call_desk_kernel(
             )
             return bf[:]
 
+        def weave_on_gpsimd(planes, width, slot):
+            bf = woven.tile([P, PACK * width], BF16, name="bf%d" % slot, align_bytes=64)
+            nc.gpsimd.tensor_scalar(
+                bf[:].rearrange("p (c j) -> p c j", j=PACK), planes.rearrange("p j c -> p c j"),
+                1.0, 0.0, ALU.mult, ALU.add,
+            )
+            return bf[:]
+
         def first_stage(passes, bias, slot):
             row = rows.tile([P, S], F32, name="row%d" % slot)
             for c in range(S // BANK):
@@ -238,9 +246,10 @@ def tile_list_emergency_call_desk_kernel(
         w4_raw.append(load_weight_block(w4, 1, 0, 0))
         for u in range(4):
             a_rows[u] = a_stage(u, 2 + u)
-        w4_q = [quantize("w4_%d" % a, weave(nc.vector.tensor_copy, w4_raw[a][:], N, 3 - a), N) for a in range(2)]
+        w4_bf = [weave_on_gpsimd(w4_raw[a][:], N, 3 - a) for a in range(2)]
         pick_max(xa0, 0, 0, J)
         xb_q = [quantize("xb_%d" % a, weave(nc.scalar.copy, xb[a][:], J, a), J) for a in range(2)]
+        w4_q = [quantize("w4_%d" % a, w4_bf[a], N) for a in range(2)]
         for u in range(4):
             pick_mult(z0, xa0, u, 0, J)
         for u, slot in zip(range(4, 8), (6, 7, 2, 3)):

@@ -19,8 +19,13 @@ ALU = mybir.AluOpType
 P = 128
 PACK = 4
 PASS = P * PACK
+QUADS = 4
 BANK = 512
+TURN_BANKS = 6
+ROW_SLOTS = 10
+LINE = 4
 HALF = J // 2
+STORES = 5
 
 
 def tile_list_emergency_call_desk_kernel(
@@ -34,32 +39,32 @@ def tile_list_emergency_call_desk_kernel(
         raws = ctx.enter_context(tc.tile_pool(name="raws", bufs=1))
         woven = ctx.enter_context(tc.tile_pool(name="woven", bufs=1))
         rows = ctx.enter_context(tc.tile_pool(name="rows", bufs=1))
-        results = ctx.enter_context(tc.tile_pool(name="results", bufs=3))
-        acc_pool = ctx.enter_context(tc.psum_pool(name="acc", bufs=1))
-        y_pool = ctx.enter_context(tc.psum_pool(name="y", bufs=2))
+        results = ctx.enter_context(tc.tile_pool(name="results", bufs=STORES))
+        psum = ctx.enter_context(tc.psum_pool(name="psum", bufs=1))
+        y1_psum = ctx.enter_context(tc.psum_pool(name="y1_psum", bufs=2))
 
-        made = {"row": 0, "acc": 0}
+        banks_taken = []
 
-        def in_turn(pool, kind, slots, shape):
-            n = made[kind]
-            made[kind] = n + 1
-            return pool.tile(shape, F32, name="%s%d" % (kind, n % slots))
+        def new_bank(shape):
+            bank = psum.tile(shape, F32, name="bank%d" % (len(banks_taken) % TURN_BANKS))
+            banks_taken.append(bank)
+            return bank
 
         def load_list(name, src):
             tile = keep.tile(list(src.shape), U16, name=name)
             nc.sync.dma_start(tile[:], src)
             return tile
 
-        def zeroed_plane(name, width):
-            plane = keep.tile([P, width], U8, name=name, align_bytes=64)
-            nc.vector.memset(plane[:].bitcast(I32), 0)
-            return plane
+        def zeroed_scale_tile(name, width):
+            tile = keep.tile([P, width], U8, name=name, align_bytes=64)
+            nc.vector.memset(tile[:].bitcast(I32), 0)
+            return tile
 
-        def load_table_scales(plane, scales):
+        def load_scale_rows(tile, scales):
             passes = scales.shape[0]
-            for q in range(4):
+            for q in range(QUADS):
                 nc.sync.dma_start(
-                    out=plane[32 * q : 32 * q + 4 * passes, :].bitcast(I32),
+                    out=tile[32 * q : 32 * q + 4 * passes, :].bitcast(I32),
                     in_=scales[:, 4 * q : 4 * q + 4, :].bitcast(I32),
                 )
 
@@ -68,21 +73,21 @@ def tile_list_emergency_call_desk_kernel(
             nc.sync.dma_start(out=tile[:], in_=words.rearrange("p t i -> p (t i)").bitcast(I32))
             return tile
 
-        def gather_words(name, words, idx):
+        def gather_words(name, words, places):
             picked = keep.tile([P, S], U32, name=name, align_bytes=64)
-            nc.vector.tensor_copy(picked[:], words[:].bitcast(U32).indirect(idx[:]))
+            nc.vector.tensor_copy(picked[:], words[:].bitcast(U32).indirect(places[:]))
             return picked
 
-        def gather_scales(name, plane, idx):
+        def gather_scales(name, scale_tile, places):
             picked = keep.tile([P, S], U8, name=name, align_bytes=64)
-            nc.vector.tensor_copy(picked[:], plane[:].indirect(idx[:]))
+            nc.vector.tensor_copy(picked[:], scale_tile[:].indirect(places[:]))
             return picked
 
-        def load_weight_block(w, a, b, slot):
+        def load_weight_block(w, g, blk, slot):
             raw = raws.tile([P, PACK, PASS], F32, name="raw%d" % slot)
             nc.sync.dma_start(
                 out=raw[:],
-                in_=w[PASS * a : PASS * (a + 1), PASS * b : PASS * (b + 1)].rearrange("(p j) c -> p j c", j=PACK),
+                in_=w[PASS * g : PASS * (g + 1), PASS * blk : PASS * (blk + 1)].rearrange("(p i) c -> p i c", i=PACK),
             )
             return raw
 
@@ -92,40 +97,32 @@ def tile_list_emergency_call_desk_kernel(
             nc.vector.quantize_mx(out=codes[:].bitcast(FP8X4), scales=scales[:], in_=bf)
             return codes, scales
 
-        def weave_dealt(raw, slot):
+        def weave_and_deal(raw, slot):
             bf = woven.tile([P, PACK * PASS], BF16, name="bf%d" % slot, align_bytes=64)
             nc.scalar.copy(
-                out=bf[:].rearrange("p (t m j) -> p m j t", t=PACK, j=PACK),
-                in_=raw[:].rearrange("p j (m t) -> p m j t", t=PACK),
+                out=bf[:].rearrange("p (t m i) -> p m i t", t=PACK, i=PACK),
+                in_=raw[:].rearrange("p i (m t) -> p m i t", t=PACK),
             )
             return bf[:]
 
         def weave(copy, planes, width, slot):
             bf = woven.tile([P, PACK * width], BF16, name="bf%d" % slot, align_bytes=64)
             copy(
-                out=bf[:].rearrange("p (c i j) -> p c j i", i=4, j=PACK),
-                in_=planes.rearrange("p j (c i) -> p c j i", i=4),
+                out=bf[:].rearrange("p (c e i) -> p c i e", e=LINE, i=PACK),
+                in_=planes.rearrange("p i (c e) -> p c i e", e=LINE),
             )
             return bf[:]
 
-        def weave_on_gpsimd(planes, width, slot):
-            bf = woven.tile([P, PACK * width], BF16, name="bf%d" % slot, align_bytes=64)
-            nc.gpsimd.tensor_scalar(
-                bf[:].rearrange("p (c j) -> p c j", j=PACK), planes.rearrange("p j c -> p c j"),
-                1.0, 0.0, ALU.mult, ALU.add,
-            )
-            return bf[:]
-
-        def first_stage(passes, bias, slot):
+        def row_tile(passes, bias, slot):
             row = rows.tile([P, S], F32, name="row%d" % slot)
             for c in range(S // BANK):
                 cols = slice(BANK * c, BANK * (c + 1))
-                acc = in_turn(acc_pool, "acc", 6, [P, BANK])
-                for n, (w_codes, w_scales, v_codes, v_scales, k) in enumerate(passes):
+                acc = new_bank([P, BANK])
+                for g, (w_codes, w_scales, v_codes, v_scales) in enumerate(passes):
                     nc.tensor.matmul_mx(
                         out=acc[:], lhsT=w_codes, lhsT_scale=w_scales,
-                        rhs=v_codes[:, cols].bitcast(FP8X4), rhs_scale=v_scales[k:P, cols],
-                        start=(n == 0), stop=(n == len(passes) - 1),
+                        rhs=v_codes[:, cols].bitcast(FP8X4), rhs_scale=v_scales[4 * g : P, cols],
+                        start=(g == 0), stop=(g == len(passes) - 1),
                     )
                 if bias is None:
                     nc.scalar.copy(out=row[:, cols], in_=acc[:])
@@ -133,179 +130,183 @@ def tile_list_emergency_call_desk_kernel(
                     nc.scalar.activation(out=row[:, cols], in_=acc[:], func=ACT.Identity, bias=bias)
             return row
 
-        def fp8_cols(q, u):
-            cols = slice(P * u, P * (u + 1))
-            return q[0][:, cols].bitcast(FP8X4), q[1][:, cols]
+        def stationary(quantized, n):
+            cols = slice(P * n, P * (n + 1))
+            return quantized[0][:, cols].bitcast(FP8X4), quantized[1][:, cols]
 
-        v2_plane = zeroed_plane("v2_plane", T)
-        w2_plane = zeroed_plane("w2_plane", H)
-        v3_plane = zeroed_plane("v3_plane", T)
-        v1_plane = zeroed_plane("v1_plane", T)
-        w5_plane = zeroed_plane("w5_plane", 2 * N)
+        v2_scale_tile = zeroed_scale_tile("v2_scale_tile", T)
+        w2_scale_tile = zeroed_scale_tile("w2_scale_tile", H)
+        v3_scale_tile = zeroed_scale_tile("v3_scale_tile", T)
+        v1_scale_tile = zeroed_scale_tile("v1_scale_tile", T)
+        w5_scale_tile = zeroed_scale_tile("w5_scale_tile", 2 * N)
 
         idx2 = load_list("idx2", offs2)
         idx3 = load_list("idx3", offs3)
         w2_raw = keep.tile([P, 2 * H], U8, name="w2_raw")
         nc.sync.dma_start(out=w2_raw[:].bitcast(I32), in_=w2_words[0].bitcast(I32))
-        load_table_scales(v2_plane, tab2_scales)
+        load_scale_rows(v2_scale_tile, tab2_scales)
         v2_words = load_table_words("v2_words", tab2_words[0])
-        w3_raw0 = load_weight_block(w3, 0, 0, 0)
-        load_table_scales(w2_plane, w2_scales)
+        w3_raw = [load_weight_block(w3, 0, 0, 0)]
+        load_scale_rows(w2_scale_tile, w2_scales)
         v3_words = load_table_words("v3_words", tab3_words[0])
-        load_table_scales(v3_plane, tab3_scales)
-        w3_raw1 = load_weight_block(w3, 0, 1, 1)
+        load_scale_rows(v3_scale_tile, tab3_scales)
+        w3_raw.append(load_weight_block(w3, 0, 1, 1))
         p2 = load_list("p2", pos2)
         v1_words = [load_table_words("v1_words0", tab_words[0])]
         idx1 = load_list("idx1", offs)
-        load_table_scales(v1_plane, tab_scales)
+        load_scale_rows(v1_scale_tile, tab_scales)
         v1_words.append(load_table_words("v1_words1", tab_words[1]))
         bd_t = keep.tile([P, 2, PACK], F32, name="bd_t")
-        nc.sync.dma_start(out=bd_t[:], in_=bd.rearrange("(a p t) -> p a t", a=2, t=PACK))
-        w1_raw = {(a, 0): load_weight_block(w1, a, 0, 2 + a) for a in range(2)}
+        nc.sync.dma_start(out=bd_t[:], in_=bd.rearrange("(g p t) -> p g t", g=2, t=PACK))
+        w1_raw = {(g, 0): load_weight_block(w1, g, 0, 2 + g) for g in range(2)}
         p1 = load_list("p1", pos1)
         p3 = load_list("p3", pos3)
 
-        v2_scales = gather_scales("v2_scales", v2_plane, idx2)
+        v2_scales = gather_scales("v2_scales", v2_scale_tile, idx2)
         w2_dealt = keep.tile([P, 2 * H], U8, name="w2_dealt", align_bytes=64)
         nc.vector.tensor_copy(
-            out=w2_dealt[:].bitcast(U16).rearrange("p (b t m) -> p b t m", b=2, t=PACK),
-            in_=w2_raw[:].bitcast(U16).rearrange("p (b m t) -> p b t m", b=2, t=PACK),
+            out=w2_dealt[:].bitcast(U16).rearrange("p (blk t m) -> p blk t m", blk=2, t=PACK),
+            in_=w2_raw[:].bitcast(U16).rearrange("p (blk m t) -> p blk t m", blk=2, t=PACK),
         )
         v2_codes = gather_words("v2_codes", v2_words, idx2)
         w2_dealt_scales = keep.tile([P, H], U8, name="w2_dealt_scales", align_bytes=64)
         nc.vector.tensor_copy(
-            out=w2_dealt_scales[:].rearrange("p (b t m) -> p b t m", b=2, t=PACK),
-            in_=w2_plane[:].rearrange("p (b m t) -> p b t m", b=2, t=PACK),
+            out=w2_dealt_scales[:].rearrange("p (blk t m) -> p blk t m", blk=2, t=PACK),
+            in_=w2_scale_tile[:].rearrange("p (blk m t) -> p blk t m", blk=2, t=PACK),
         )
-        w3_bf = [weave_dealt(w3_raw0, 0), weave_dealt(w3_raw1, 1)]
-        for a in range(2):
-            w1_raw[(a, 1)] = load_weight_block(w1, a, 1, a)
+        w3_bf = [weave_and_deal(w3_raw[blk], blk) for blk in range(2)]
+
+        for g in range(2):
+            w1_raw[(g, 1)] = load_weight_block(w1, g, 1, g)
         w5_codes = keep.tile([P, 2, 2 * N], U8, name="w5_codes", align_bytes=64)
-        nc.sync.dma_start(out=w5_codes[:].bitcast(I32), in_=w5_words.rearrange("a p c -> p a c").bitcast(I32))
-        for q in range(4):
+        nc.sync.dma_start(out=w5_codes[:].bitcast(I32), in_=w5_words.rearrange("g p c -> p g c").bitcast(I32))
+        for q in range(QUADS):
             nc.sync.dma_start(
-                out=w5_plane[32 * q : 32 * q + 4, :].rearrange("r (a n) -> r a n", a=2).bitcast(I32),
-                in_=w5_scales[:, 4 * q : 4 * q + 4, :].rearrange("a r n -> r a n").bitcast(I32),
+                out=w5_scale_tile[32 * q : 32 * q + 4, :].rearrange("r (g n) -> r g n", g=2).bitcast(I32),
+                in_=w5_scales[:, 4 * q : 4 * q + 4, :].rearrange("g r n -> r g n").bitcast(I32),
             )
         ge_t = keep.tile([P, N // P], F32, name="ge_t")
-        with nc.allow_non_contiguous_dma(reason="one gain a partition"):
-            nc.sync.dma_start(out=ge_t[:], in_=ge.rearrange("(i p) -> p i", p=P))
+        with nc.allow_non_contiguous_dma(reason="one gain for each output row"):
+            nc.sync.dma_start(out=ge_t[:], in_=ge.rearrange("(n p) -> p n", p=P))
 
         b_rows = [
-            first_stage(
+            row_tile(
                 [(w2_dealt[:, 2 * P * u : 2 * P * (u + 1)].bitcast(FP4X4), w2_dealt_scales[:, P * u : P * (u + 1)],
-                  v2_codes, v2_scales, 0)],
+                  v2_codes, v2_scales)],
                 None, u,
             )
-            for u in range(8)
+            for u in range(H // P)
         ]
 
-        v3_scales = gather_scales("v3_scales", v3_plane, idx3)
+        v3_scales = gather_scales("v3_scales", v3_scale_tile, idx3)
         v3_codes = gather_words("v3_codes", v3_words, idx3)
-        w3_q = [quantize("w3_%d" % b, w3_bf[b], PASS) for b in range(2)]
-        v1_scales = gather_scales("v1_scales", v1_plane, idx1)
-        v1_codes = [gather_words("v1_codes%d" % a, v1_words[a], idx1) for a in range(2)]
+        w3_q = [quantize("w3_%d" % blk, w3_bf[blk], PASS) for blk in range(2)]
+        v1_scales = gather_scales("v1_scales", v1_scale_tile, idx1)
+        v1_codes = [gather_words("v1_codes%d" % g, v1_words[g], idx1) for g in range(2)]
 
-        w1_q = {}
-        for a in range(2):
-            w1_q[(a, 0)] = quantize("w1_%d0" % a, weave_dealt(w1_raw[(a, 0)], 2 + a), PASS)
+        w1_q = {(g, 0): quantize("w1_%d0" % g, weave_and_deal(w1_raw[(g, 0)], 2 + g), PASS) for g in range(2)}
         w4_raw = [load_weight_block(w4, 0, 0, 2)]
 
         xb = [keep.tile([P, PACK, J], F32, name="xb0"), raws.tile([P, PACK, J], F32, name="raw3")]
-        for u in range(8):
+        for u in range(H // P):
             nc.vector.tensor_copy(xb[u // PACK][:, u % PACK, :], b_rows[u][:].indirect(p2[:]))
 
-        def d_stage(u, slot):
-            b, t = divmod(u, PACK)
-            return first_stage([fp8_cols(w3_q[b], t) + (v3_codes, v3_scales, 0)], bd_t[:, b, t : t + 1], slot)
+        def d_rows(blk, slots):
+            return [row_tile([stationary(w3_q[blk], t) + (v3_codes, v3_scales)], bd_t[:, blk, t : t + 1], slots[t])
+                    for t in range(PACK)]
 
-        def a_stage(u, slot):
-            b, t = divmod(u, PACK)
-            return first_stage(
-                [fp8_cols(w1_q[(a, b)], t) + (v1_codes[a], v1_scales, 4 * a) for a in range(2)], None, slot
-            )
+        def a_rows(blk, slots):
+            return [
+                row_tile([stationary(w1_q[(g, blk)], t) + (v1_codes[g], v1_scales) for g in range(2)], None, slots[t])
+                for t in range(PACK)
+            ]
 
-        def pick_max(xa, b, j0, width):
+        freed = list(range(H // P, ROW_SLOTS)) + list(range(H // P))
+        d0_slots, a0_slots = freed[:PACK], freed[PACK : 2 * PACK]
+        freed = freed[2 * PACK :] + a0_slots + d0_slots
+        a1_slots, d1_slots = freed[:PACK], freed[PACK : 2 * PACK]
+
+        def pick_max(larger, a_tiles, g):
             for t in range(PACK):
-                nc.vector.tensor_copy(xa[:, t, :], a_rows[PACK * b + t][:].indirect(p1[:, j0 // 16 : (j0 + width) // 16]))
-            nc.vector.tensor_tensor(xa[:], xa[:], xb[b][:, :, j0 : j0 + width], ALU.max)
+                nc.vector.tensor_copy(larger[:, t, :], a_tiles[t][:].indirect(p1[:]))
+            nc.vector.tensor_tensor(larger[:], larger[:], xb[g][:], ALU.max)
 
-        def pick_mult(z, xa, u, j0, width):
-            t = u % PACK
-            nc.vector.tensor_tensor(
-                z[:, t, :], d_rows[u][:].indirect(p3[:, j0 // 16 : (j0 + width) // 16]), xa[:, t, j0 : j0 + width], ALU.mult
-            )
+        def pick_mult(z, larger, d_tiles, cols):
+            places = p3[:, cols.start // 16 : cols.stop // 16]
+            for t in range(PACK):
+                nc.vector.tensor_tensor(z[:, t, :], d_tiles[t][:].indirect(places), larger[:, t, cols], ALU.mult)
 
         z0 = keep.tile([P, PACK, J], F32, name="z0")
-        xa0 = keep.tile([P, PACK, J], F32, name="xa")
-        a_rows, d_rows = {}, {}
-        for u, slot in zip(range(4), (8, 9, 0, 1)):
-            d_rows[u] = d_stage(u, slot)
-        for a in range(2):
-            w1_q[(a, 1)] = quantize("w1_%d1" % a, weave_dealt(w1_raw[(a, 1)], a), PASS)
+        larger0 = keep.tile([P, PACK, J], F32, name="larger")
+        d0 = d_rows(0, d0_slots)
+        for g in range(2):
+            w1_q[(g, 1)] = quantize("w1_%d1" % g, weave_and_deal(w1_raw[(g, 1)], g), PASS)
         w4_raw.append(load_weight_block(w4, 1, 0, 0))
-        for u in range(4):
-            a_rows[u] = a_stage(u, 2 + u)
-        w4_bf = [weave_on_gpsimd(w4_raw[a][:], N, 3 - a) for a in range(2)]
-        pick_max(xa0, 0, 0, J)
-        xb_q = [quantize("xb_%d" % a, weave(nc.scalar.copy, xb[a][:], J, a), J) for a in range(2)]
-        w4_q = [quantize("w4_%d" % a, w4_bf[a], N) for a in range(2)]
-        for u in range(4):
-            pick_mult(z0, xa0, u, 0, J)
-        for u, slot in zip(range(4, 8), (6, 7, 2, 3)):
-            a_rows[u] = a_stage(u, slot)
-        xa1 = keep.tile([P, PACK, J], F32, name="xa")
-        pick_max(xa1, 1, 0, J)
-        for u, slot in zip(range(4, 8), (4, 5, 8, 9)):
-            d_rows[u] = d_stage(u, slot)
-        y2 = keep.tile([P, N // P, J], F32, name="y2")
-        for i in range(N // P):
-            acc = in_turn(acc_pool, "acc", 6, [P, BANK])
-            for a in range(2):
-                nc.tensor.matmul_mx(
-                    out=acc[:],
-                    lhsT=w5_codes[:, a, 2 * P * i : 2 * P * (i + 1)].bitcast(FP4X4),
-                    lhsT_scale=w5_plane[:, N * a + P * i : N * a + P * (i + 1)],
-                    rhs=xb_q[a][0][:].bitcast(FP8X4), rhs_scale=xb_q[a][1][:],
-                    start=(a == 0), stop=(a == 1),
-                )
-            nc.scalar.activation(out=y2[:, i, :], in_=acc[:], func=ACT.Copy, scale=ge_t[:, i : i + 1])
+        pick_max(larger0, a_rows(0, a0_slots), 0)
+        xb_q = [quantize("xb_%d" % g, weave(nc.scalar.copy, xb[g][:], J, g), J) for g in range(2)]
+        w4_q = [quantize("w4_%d" % g, weave(nc.scalar.copy, w4_raw[g][:], N, 3 - g), N) for g in range(2)]
+        pick_mult(z0, larger0, d0, slice(0, J))
 
+        a1 = a_rows(1, a1_slots)
+        larger1 = keep.tile([P, PACK, J], F32, name="larger")
+        pick_max(larger1, a1, 1)
+        d1 = d_rows(1, d1_slots)
+
+        gained = keep.tile([P, N // P, J], F32, name="gained")
+
+        def y2_tiles(pair):
+            for n in (2 * pair, 2 * pair + 1):
+                acc = new_bank([P, BANK])
+                for g in range(2):
+                    nc.tensor.matmul_mx(
+                        out=acc[:],
+                        lhsT=w5_codes[:, g, 2 * P * n : 2 * P * (n + 1)].bitcast(FP4X4),
+                        lhsT_scale=w5_scale_tile[:, N * g + P * n : N * g + P * (n + 1)],
+                        rhs=xb_q[g][0][:].bitcast(FP8X4), rhs_scale=xb_q[g][1][:],
+                        start=(g == 0), stop=(g == 1),
+                    )
+                nc.scalar.activation(out=gained[:, n, :], in_=acc[:], func=ACT.Copy, scale=ge_t[:, n : n + 1])
+
+        halves = [slice(HALF * h, HALF * (h + 1)) for h in range(2)]
+        y2_tiles(0)
         z0_q = quantize("z0", weave(nc.scalar.copy, z0[:], J, 3), J)
         z1 = [keep.tile([P, PACK, HALF], F32, name="z1"), keep.tile([P, PACK, HALF], F32, name="z0")]
-        for u in range(4, 8):
-            pick_mult(z1[0], xa1, u, 0, HALF)
+        pick_mult(z1[0], larger1, d1, halves[0])
         z1_q = [quantize("z1_0", weave(nc.scalar.copy, z1[0][:], HALF, 0), HALF)]
-        for u in range(4, 8):
-            pick_mult(z1[1], xa1, u, HALF, HALF)
+        y2_tiles(1)
+        pick_mult(z1[1], larger1, d1, halves[1])
         last_bf = weave(nc.vector.tensor_copy, z1[1][:], HALF, 1)
-        out_v = out.rearrange("(i p) j -> p i j", p=P)
+        out_v = out.rearrange("(n p) j -> p n j", p=P)
 
-        def finish(h, pair):
-            cols = slice(HALF * h, HALF * (h + 1))
-            if True:
-                y1 = y_pool.tile([P, 2, HALF], F32, name="y1")
-                for e in range(2):
-                    i = 2 * pair + e
-                    w_codes, w_scales = fp8_cols(w4_q[0], i)
-                    nc.tensor.matmul_mx(
-                        out=y1[:, e, :], lhsT=w_codes, lhsT_scale=w_scales,
-                        rhs=z0_q[0][:, cols].bitcast(FP8X4), rhs_scale=z0_q[1][:, cols],
-                        start=True, stop=False,
-                    )
-                    w_codes, w_scales = fp8_cols(w4_q[1], i)
-                    nc.tensor.matmul_mx(
-                        out=y1[:, e, :], lhsT=w_codes, lhsT_scale=w_scales,
-                        rhs=z1_q[h][0][:].bitcast(FP8X4), rhs_scale=z1_q[h][1][:],
-                        start=False, stop=True,
-                    )
-                diff = results.tile([P, 2, HALF], F32, name="diff")
-                nc.vector.tensor_tensor(diff[:], y1[:], y2[:, 2 * pair : 2 * pair + 2, cols], ALU.subtract)
+        def y1_pass(bank, g, pair, z_codes, z_scales):
+            for e in range(2):
+                w_codes, w_scales = stationary(w4_q[g], 2 * pair + e)
+                nc.tensor.matmul_mx(
+                    out=bank[:, e, :], lhsT=w_codes, lhsT_scale=w_scales,
+                    rhs=z_codes.bitcast(FP8X4), rhs_scale=z_scales,
+                    start=(g == 0 and e == 0), stop=(g == 1 and e == 1),
+                )
+
+        def finish(h, pair, pieces):
+            y1_pass(y1[(h, pair)], 1, pair, z1_q[h][0][:], z1_q[h][1][:])
+            for e0, e1 in pieces:
+                tiles = slice(2 * pair + e0, 2 * pair + e1)
+                diff = results.tile([P, e1 - e0, HALF], F32, name="diff")
+                nc.vector.tensor_tensor(diff[:], y1[(h, pair)][:, e0:e1, :], gained[:, tiles, halves[h]], ALU.subtract)
                 nc.scalar.activation(out=diff[:], in_=diff[:], func=ACT.Square)
-                nc.sync.dma_start(out=out_v[:, 2 * pair : 2 * pair + 2, cols], in_=diff[:])
+                nc.sync.dma_start(out=out_v[:, tiles, halves[h]], in_=diff[:])
 
-        finish(0, 0)
+        y1 = {}
+        for h in range(2):
+            for pair in range(2):
+                if h == 0:
+                    y1[(h, pair)] = y1_psum.tile([P, 2, HALF], F32, name="y1")
+                else:
+                    y1[(h, pair)] = new_bank([P, 2, HALF])
+                y1_pass(y1[(h, pair)], 0, pair, z0_q[0][:, halves[h]], z0_q[1][:, halves[h]])
+
+        finish(0, 0, [(0, 2)])
         z1_q.append(quantize("z1_1", last_bf, HALF))
-        finish(0, 1)
-        for pair in range(2):
-            finish(1, pair)
+        finish(0, 1, [(0, 2)])
+        finish(1, 0, [(0, 2)])
+        finish(1, 1, [(0, 1), (1, 2)])

from contextlib import ExitStack

import concourse.mybir as mybir

K, K2, H, N, T, S, J = 1024, 512, 1024, 512, 2048, 1024, 512
FLOPS = 2 * (K * H * S + 2 * K2 * H * S + 2 * H * N * J)

F32 = mybir.dt.float32
BF16 = mybir.dt.bfloat16
I32 = mybir.dt.int32
U32 = mybir.dt.uint32
U16 = mybir.dt.uint16
U8 = mybir.dt.uint8
FP8X4 = mybir.dt.float8_e4m3fn_x4
FP4X4 = mybir.dt.float4_e2m1fn_x4
ACT = mybir.ActivationFunctionType
ALU = mybir.AluOpType

P = 128
PACK = 4
PASS = P * PACK
QUADS = 4
BANK = 512
TURN_BANKS = 6
ROW_SLOTS = 10
LINE = 4
HALF = J // 2
STORES = 5


def tile_list_emergency_call_desk_kernel(
    tc, tab_words, tab_scales, tab2_words, tab2_scales, tab3_words, tab3_scales,
    offs, offs2, offs3, pos1, pos2, pos3, w1, w2_words, w2_scales, w3, bd, w4,
    w5_words, w5_scales, ge, out,
):
    nc = tc.nc
    with ExitStack() as ctx:
        keep = ctx.enter_context(tc.tile_pool(name="keep", bufs=1))
        raws = ctx.enter_context(tc.tile_pool(name="raws", bufs=1))
        woven = ctx.enter_context(tc.tile_pool(name="woven", bufs=1))
        rows = ctx.enter_context(tc.tile_pool(name="rows", bufs=1))
        results = ctx.enter_context(tc.tile_pool(name="results", bufs=STORES))
        psum = ctx.enter_context(tc.psum_pool(name="psum", bufs=1))
        y1_psum = ctx.enter_context(tc.psum_pool(name="y1_psum", bufs=2))

        banks_taken = []

        def new_bank(shape):
            bank = psum.tile(shape, F32, name="bank%d" % (len(banks_taken) % TURN_BANKS))
            banks_taken.append(bank)
            return bank

        def load_list(name, src):
            tile = keep.tile(list(src.shape), U16, name=name)
            nc.sync.dma_start(tile[:], src)
            return tile

        def zeroed_scale_tile(name, width):
            tile = keep.tile([P, width], U8, name=name, align_bytes=64)
            nc.vector.memset(tile[:].bitcast(I32), 0)
            return tile

        def load_scale_rows(tile, scales):
            passes = scales.shape[0]
            for q in range(QUADS):
                nc.sync.dma_start(
                    out=tile[32 * q : 32 * q + 4 * passes, :].bitcast(I32),
                    in_=scales[:, 4 * q : 4 * q + 4, :].bitcast(I32),
                )

        def load_table_words(name, words):
            tile = keep.tile([P, T], I32, name=name)
            nc.sync.dma_start(out=tile[:], in_=words.rearrange("p t i -> p (t i)").bitcast(I32))
            return tile

        def gather_words(name, words, places):
            picked = keep.tile([P, S], U32, name=name, align_bytes=64)
            nc.vector.tensor_copy(picked[:], words[:].bitcast(U32).indirect(places[:]))
            return picked

        def gather_scales(name, scale_tile, places):
            picked = keep.tile([P, S], U8, name=name, align_bytes=64)
            nc.vector.tensor_copy(picked[:], scale_tile[:].indirect(places[:]))
            return picked

        def load_weight_block(w, g, blk, slot):
            raw = raws.tile([P, PACK, PASS], F32, name="raw%d" % slot)
            nc.sync.dma_start(
                out=raw[:],
                in_=w[PASS * g : PASS * (g + 1), PASS * blk : PASS * (blk + 1)].rearrange("(p i) c -> p i c", i=PACK),
            )
            return raw

        def quantize(name, bf, width):
            codes = keep.tile([P, width], U32, name=name + "_codes", align_bytes=64)
            scales = keep.tile([P, width], U8, name=name + "_scales", align_bytes=64)
            nc.vector.quantize_mx(out=codes[:].bitcast(FP8X4), scales=scales[:], in_=bf)
            return codes, scales

        def weave_and_deal(raw, slot):
            bf = woven.tile([P, PACK * PASS], BF16, name="bf%d" % slot, align_bytes=64)
            nc.scalar.copy(
                out=bf[:].rearrange("p (t m i) -> p m i t", t=PACK, i=PACK),
                in_=raw[:].rearrange("p i (m t) -> p m i t", t=PACK),
            )
            return bf[:]

        def weave(copy, planes, width, slot):
            bf = woven.tile([P, PACK * width], BF16, name="bf%d" % slot, align_bytes=64)
            copy(
                out=bf[:].rearrange("p (c e i) -> p c i e", e=LINE, i=PACK),
                in_=planes.rearrange("p i (c e) -> p c i e", e=LINE),
            )
            return bf[:]

        def row_tile(passes, bias, slot):
            row = rows.tile([P, S], F32, name="row%d" % slot)
            for c in range(S // BANK):
                cols = slice(BANK * c, BANK * (c + 1))
                acc = new_bank([P, BANK])
                for g, (w_codes, w_scales, v_codes, v_scales) in enumerate(passes):
                    nc.tensor.matmul_mx(
                        out=acc[:], lhsT=w_codes, lhsT_scale=w_scales,
                        rhs=v_codes[:, cols].bitcast(FP8X4), rhs_scale=v_scales[4 * g : P, cols],
                        start=(g == 0), stop=(g == len(passes) - 1),
                    )
                if bias is None:
                    nc.scalar.copy(out=row[:, cols], in_=acc[:])
                else:
                    nc.scalar.activation(out=row[:, cols], in_=acc[:], func=ACT.Identity, bias=bias)
            return row

        def stationary(quantized, n):
            cols = slice(P * n, P * (n + 1))
            return quantized[0][:, cols].bitcast(FP8X4), quantized[1][:, cols]

        v2_scale_tile = zeroed_scale_tile("v2_scale_tile", T)
        w2_scale_tile = zeroed_scale_tile("w2_scale_tile", H)
        v3_scale_tile = zeroed_scale_tile("v3_scale_tile", T)
        v1_scale_tile = zeroed_scale_tile("v1_scale_tile", T)
        w5_scale_tile = zeroed_scale_tile("w5_scale_tile", 2 * N)

        idx2 = load_list("idx2", offs2)
        idx3 = load_list("idx3", offs3)
        w2_raw = keep.tile([P, 2 * H], U8, name="w2_raw")
        nc.sync.dma_start(out=w2_raw[:].bitcast(I32), in_=w2_words[0].bitcast(I32))
        load_scale_rows(v2_scale_tile, tab2_scales)
        v2_words = load_table_words("v2_words", tab2_words[0])
        w3_raw = [load_weight_block(w3, 0, 0, 0)]
        load_scale_rows(w2_scale_tile, w2_scales)
        v3_words = load_table_words("v3_words", tab3_words[0])
        load_scale_rows(v3_scale_tile, tab3_scales)
        w3_raw.append(load_weight_block(w3, 0, 1, 1))
        p2 = load_list("p2", pos2)
        v1_words = [load_table_words("v1_words0", tab_words[0])]
        idx1 = load_list("idx1", offs)
        load_scale_rows(v1_scale_tile, tab_scales)
        v1_words.append(load_table_words("v1_words1", tab_words[1]))
        bd_t = keep.tile([P, 2, PACK], F32, name="bd_t")
        nc.sync.dma_start(out=bd_t[:], in_=bd.rearrange("(g p t) -> p g t", g=2, t=PACK))
        w1_raw = {(g, 0): load_weight_block(w1, g, 0, 2 + g) for g in range(2)}
        p1 = load_list("p1", pos1)
        p3 = load_list("p3", pos3)

        v2_scales = gather_scales("v2_scales", v2_scale_tile, idx2)
        w2_dealt = keep.tile([P, 2 * H], U8, name="w2_dealt", align_bytes=64)
        nc.vector.tensor_copy(
            out=w2_dealt[:].bitcast(U16).rearrange("p (blk t m) -> p blk t m", blk=2, t=PACK),
            in_=w2_raw[:].bitcast(U16).rearrange("p (blk m t) -> p blk t m", blk=2, t=PACK),
        )
        v2_codes = gather_words("v2_codes", v2_words, idx2)
        w2_dealt_scales = keep.tile([P, H], U8, name="w2_dealt_scales", align_bytes=64)
        nc.vector.tensor_copy(
            out=w2_dealt_scales[:].rearrange("p (blk t m) -> p blk t m", blk=2, t=PACK),
            in_=w2_scale_tile[:].rearrange("p (blk m t) -> p blk t m", blk=2, t=PACK),
        )
        w3_bf = [weave_and_deal(w3_raw[blk], blk) for blk in range(2)]

        for g in range(2):
            w1_raw[(g, 1)] = load_weight_block(w1, g, 1, g)
        w5_codes = keep.tile([P, 2, 2 * N], U8, name="w5_codes", align_bytes=64)
        nc.sync.dma_start(out=w5_codes[:].bitcast(I32), in_=w5_words.rearrange("g p c -> p g c").bitcast(I32))
        for q in range(QUADS):
            nc.sync.dma_start(
                out=w5_scale_tile[32 * q : 32 * q + 4, :].rearrange("r (g n) -> r g n", g=2).bitcast(I32),
                in_=w5_scales[:, 4 * q : 4 * q + 4, :].rearrange("g r n -> r g n").bitcast(I32),
            )
        ge_t = keep.tile([P, N // P], F32, name="ge_t")
        with nc.allow_non_contiguous_dma(reason="one gain for each output row"):
            nc.sync.dma_start(out=ge_t[:], in_=ge.rearrange("(n p) -> p n", p=P))

        b_rows = [
            row_tile(
                [(w2_dealt[:, 2 * P * u : 2 * P * (u + 1)].bitcast(FP4X4), w2_dealt_scales[:, P * u : P * (u + 1)],
                  v2_codes, v2_scales)],
                None, u,
            )
            for u in range(H // P)
        ]

        v3_scales = gather_scales("v3_scales", v3_scale_tile, idx3)
        v3_codes = gather_words("v3_codes", v3_words, idx3)
        w3_q = [quantize("w3_%d" % blk, w3_bf[blk], PASS) for blk in range(2)]
        v1_scales = gather_scales("v1_scales", v1_scale_tile, idx1)
        v1_codes = [gather_words("v1_codes%d" % g, v1_words[g], idx1) for g in range(2)]

        w1_q = {(g, 0): quantize("w1_%d0" % g, weave_and_deal(w1_raw[(g, 0)], 2 + g), PASS) for g in range(2)}
        w4_raw = [load_weight_block(w4, 0, 0, 2)]

        xb = [keep.tile([P, PACK, J], F32, name="xb0"), raws.tile([P, PACK, J], F32, name="raw3")]
        for u in range(H // P):
            nc.vector.tensor_copy(xb[u // PACK][:, u % PACK, :], b_rows[u][:].indirect(p2[:]))

        def d_rows(blk, slots):
            return [row_tile([stationary(w3_q[blk], t) + (v3_codes, v3_scales)], bd_t[:, blk, t : t + 1], slots[t])
                    for t in range(PACK)]

        def a_rows(blk, slots):
            return [
                row_tile([stationary(w1_q[(g, blk)], t) + (v1_codes[g], v1_scales) for g in range(2)], None, slots[t])
                for t in range(PACK)
            ]

        freed = list(range(H // P, ROW_SLOTS)) + list(range(H // P))
        d0_slots, a0_slots = freed[:PACK], freed[PACK : 2 * PACK]
        freed = freed[2 * PACK :] + a0_slots + d0_slots
        a1_slots, d1_slots = freed[:PACK], freed[PACK : 2 * PACK]

        def pick_max(larger, a_tiles, g):
            for t in range(PACK):
                nc.vector.tensor_copy(larger[:, t, :], a_tiles[t][:].indirect(p1[:]))
            nc.vector.tensor_tensor(larger[:], larger[:], xb[g][:], ALU.max)

        def pick_mult(z, larger, d_tiles, cols):
            places = p3[:, cols.start // 16 : cols.stop // 16]
            for t in range(PACK):
                nc.vector.tensor_tensor(z[:, t, :], d_tiles[t][:].indirect(places), larger[:, t, cols], ALU.mult)

        z0 = keep.tile([P, PACK, J], F32, name="z0")
        larger0 = keep.tile([P, PACK, J], F32, name="larger")
        d0 = d_rows(0, d0_slots)
        for g in range(2):
            w1_q[(g, 1)] = quantize("w1_%d1" % g, weave_and_deal(w1_raw[(g, 1)], g), PASS)
        w4_raw.append(load_weight_block(w4, 1, 0, 0))
        pick_max(larger0, a_rows(0, a0_slots), 0)
        xb_q = [quantize("xb_%d" % g, weave(nc.scalar.copy, xb[g][:], J, g), J) for g in range(2)]
        w4_q = [quantize("w4_%d" % g, weave(nc.scalar.copy, w4_raw[g][:], N, 3 - g), N) for g in range(2)]
        pick_mult(z0, larger0, d0, slice(0, J))

        a1 = a_rows(1, a1_slots)
        larger1 = keep.tile([P, PACK, J], F32, name="larger")
        pick_max(larger1, a1, 1)
        d1 = d_rows(1, d1_slots)

        gained = keep.tile([P, N // P, J], F32, name="gained")

        def y2_tiles(pair):
            for n in (2 * pair, 2 * pair + 1):
                acc = new_bank([P, BANK])
                for g in range(2):
                    nc.tensor.matmul_mx(
                        out=acc[:],
                        lhsT=w5_codes[:, g, 2 * P * n : 2 * P * (n + 1)].bitcast(FP4X4),
                        lhsT_scale=w5_scale_tile[:, N * g + P * n : N * g + P * (n + 1)],
                        rhs=xb_q[g][0][:].bitcast(FP8X4), rhs_scale=xb_q[g][1][:],
                        start=(g == 0), stop=(g == 1),
                    )
                nc.scalar.activation(out=gained[:, n, :], in_=acc[:], func=ACT.Copy, scale=ge_t[:, n : n + 1])

        halves = [slice(HALF * h, HALF * (h + 1)) for h in range(2)]
        y2_tiles(0)
        z0_q = quantize("z0", weave(nc.scalar.copy, z0[:], J, 3), J)
        z1 = [keep.tile([P, PACK, HALF], F32, name="z1"), keep.tile([P, PACK, HALF], F32, name="z0")]
        pick_mult(z1[0], larger1, d1, halves[0])
        z1_q = [quantize("z1_0", weave(nc.scalar.copy, z1[0][:], HALF, 0), HALF)]
        y2_tiles(1)
        pick_mult(z1[1], larger1, d1, halves[1])
        last_bf = weave(nc.vector.tensor_copy, z1[1][:], HALF, 1)
        out_v = out.rearrange("(n p) j -> p n j", p=P)

        def y1_pass(bank, g, pair, z_codes, z_scales):
            for e in range(2):
                w_codes, w_scales = stationary(w4_q[g], 2 * pair + e)
                nc.tensor.matmul_mx(
                    out=bank[:, e, :], lhsT=w_codes, lhsT_scale=w_scales,
                    rhs=z_codes.bitcast(FP8X4), rhs_scale=z_scales,
                    start=(g == 0 and e == 0), stop=(g == 1 and e == 1),
                )

        def finish(h, pair, pieces):
            y1_pass(y1[(h, pair)], 1, pair, z1_q[h][0][:], z1_q[h][1][:])
            for e0, e1 in pieces:
                tiles = slice(2 * pair + e0, 2 * pair + e1)
                diff = results.tile([P, e1 - e0, HALF], F32, name="diff")
                nc.vector.tensor_tensor(diff[:], y1[(h, pair)][:, e0:e1, :], gained[:, tiles, halves[h]], ALU.subtract)
                nc.scalar.activation(out=diff[:], in_=diff[:], func=ACT.Square)
                nc.sync.dma_start(out=out_v[:, tiles, halves[h]], in_=diff[:])

        y1 = {}
        for h in range(2):
            for pair in range(2):
                if h == 0:
                    y1[(h, pair)] = y1_psum.tile([P, 2, HALF], F32, name="y1")
                else:
                    y1[(h, pair)] = new_bank([P, 2, HALF])
                y1_pass(y1[(h, pair)], 0, pair, z0_q[0][:, halves[h]], z0_q[1][:, halves[h]])

        finish(0, 0, [(0, 2)])
        z1_q.append(quantize("z1_1", last_bf, HALF))
        finish(0, 1, [(0, 2)])
        finish(1, 0, [(0, 2)])
        finish(1, 1, [(0, 1), (1, 2)])
